import numpy as np, ml_dtypes
CORES = [16,17,18,19,150,151]
N = 6
VB, TK = 2, 256
def setup_inputs(rng):
    h = rng.standard_normal((128, TK), dtype=np.float32) / 4; w = rng.standard_normal((N, 128, VB * 128), dtype=np.float32)
    a = 2 * np.pi * rng.random((TK)); s = 400 * rng.random((TK)) ** 1.5; h[0] = s * np.cos(a); h[1] = s * np.sin(a); h[2] = 150 * rng.standard_normal((TK)); w[:, 2, :] = 1 + w[:, 2, :] / 50
    a = (2 * np.pi * rng.random() + np.pi / 2 * (rng.permutation(N).reshape(N, 1, 1) + 0.5) / N - 0.5 + (np.arange(VB).reshape(1, VB, 1) + rng.random((N, VB, 128))) / VB).reshape(N, VB * 128); w[:, 0, :] = np.cos(a); w[:, 1, :] = np.sin(a)
    tgt = rng.integers(0, N * VB * 128, size=TK)
    oh = np.zeros((N * VB * 128, TK), np.float32); oh[tgt, np.arange(TK)] = 1.0
    oh = oh.reshape(N, VB, 128, TK).transpose(0, 2, 1, 3).reshape(N, 128, VB * TK)
    return {"h": np.broadcast_to(h, (N, 128, TK)).astype(ml_dtypes.bfloat16), "w": w.astype(ml_dtypes.bfloat16), "oh": oh.astype(ml_dtypes.bfloat16)}
def reference(h, w, oh):
    H, W, OH = h.astype(np.float64), w.astype(np.float64), oh.astype(np.float64)
    Z = np.concatenate([W[r].T @ H[r] for r in range(N)], axis=0)
    O = np.concatenate([OH[r][:, TK * b:TK * b + TK] for r in range(N) for b in range(VB)], axis=0)
    m = Z.max(axis=0)
    P = np.exp(Z - m); P = P / P.sum(axis=0)
    G = P - O
    d = sum(W[r] @ G[VB * 128 * r:VB * 128 * (r + 1)] for r in range(N)).astype(ml_dtypes.bfloat16)
    return {"d": np.broadcast_to(d, (N,) + d.shape)}

@@ -1,0 +1,271 @@
+from concourse.bass import DstId, RemoteDMATransfer
+from concourse.mybir import AluOpType, AxisListType, ActivationFunctionType
+
+SLOT = 520
+NEV = 72
+SCRATCH = {
+    "hs": ("sbuf", [128, 256], "bfloat16"),
+    "ws": ("sbuf", [128, 256], "bfloat16"),
+    "ohs": ("sbuf", [128, 512], "bfloat16"),
+    "ramp": ("sbuf", [128, 128], "float32"),
+    "ident": ("sbuf", [128, 128], "bfloat16"),
+    "nident": ("sbuf", [128, 128], "bfloat16"),
+    "eT": ("sbuf", [128, 512], "bfloat16"),
+    "sacc": ("sbuf", [128, 2], "float32"),
+    "wT": ("sbuf", [128, 256], "bfloat16"),
+    "e": ("sbuf", [128, 512], "bfloat16"),
+    "pay": ("sbuf", [128, 6 * SLOT], "bfloat16"),
+    "nM": ("sbuf", [128, 2], "float32"),
+    "E": ("sbuf", [128, 12], "float32"),
+    "Tm": ("sbuf", [128, 12], "float32"),
+    "S": ("sbuf", [128, 2], "float32"),
+    "Rc": ("sbuf", [128, 2], "float32"),
+    "dg": ("sbuf", [128, 512], "bfloat16"),
+    "snd": ("sbuf", [128, 256], "bfloat16"),
+    "rcv": ("sbuf", [128, 256], "bfloat16"),
+    "prt": ("sbuf", [128, 128], "bfloat16"),
+    "dout": ("sbuf", [128, 256], "bfloat16"),
+    "p0": ("psum", [128, 512], "float32"),
+    "p1": ("psum", [128, 512], "float32"),
+    "p2": ("psum", [128, 1024], "bfloat16"),
+    "p3": ("psum", [128, 1024], "bfloat16"),
+    "p4": ("psum", [128, 1024], "bfloat16"),
+    "p5": ("psum", [128, 512], "float32"),
+    "p6": ("psum", [128, 512], "float32"),
+    "p7": ("psum", [128, 512], "float32"),
+}
+SEMAPHORES = ["a1", "a2", "ls"] + ["e%d" % i for i in range(NEV)]
+
+O_COL = (0, 388)
+U_COL = (128, 260)
+ST = 256
+
+
+def _bits(m):
+    return bin(m).count("1")
+
+
+def rank_program(g, core, T, topo):
+    rank = T.rank_of(core)
+    if rank is None:
+        return
+    cores = list(T.cores)
+    n = len(cores)
+    Exp, Square, Copy = ActivationFunctionType.Exp, ActivationFunctionType.Square, ActivationFunctionType.Copy
+    X = AxisListType.X
+
+    def place(r):
+        return (topo.host(cores[r]), topo.chip(cores[r]))
+
+    def mine_of(r):
+        return [q for q in range(n) if place(q) == place(r)]
+
+    def other_of(r):
+        return [q for q in range(n) if place(q) != place(r)]
+
+    def half(r):
+        return len(mine_of(r)) == 2 * len(other_of(r))
+
+    def blocks_of(r):
+        return [mine_of(r).index(r) % 2] if half(r) else [0, 1]
+
+    def masks(r):
+        off = topo.mask(cores[r], cores[other_of(r)[0]])
+        on = topo.mask(cores[r], cores[[q for q in mine_of(r) if q != r][0]])
+        return off, on & ~off, on & off
+
+    def pay_plan(r):
+        by = {}
+        for q in mine_of(r):
+            if q != r:
+                bl = blocks_of(q)
+                rng = (0, 516) if len(bl) == 2 else ((0, 258) if bl[0] == 0 else (258, 516))
+                by.setdefault(rng, []).append(q)
+        items = sorted(by.items(), key=lambda kv: -len(kv[1]))
+        off, stay, both = masks(r)
+        return [(rng[0], rng[1], qs, (stay, both)[i]) for i, (rng, qs) in enumerate(items)]
+
+    def d_plan(r):
+        off, stay, both = masks(r)
+        i = mine_of(r).index(r)
+        if half(r):
+            b = i % 2
+            return [(128, "rcv", 128 * b, [other_of(r)[i // 2]], off), (128, "prt", 0, [mine_of(r)[i ^ 1]], stay)]
+        return [(256, "rcv", 0, other_of(r)[2 * i:2 * i + 2], off)]
+
+    mine, other, myb = mine_of(rank), other_of(rank), blocks_of(rank)
+    nb = len(myb)
+    base = SLOT * rank
+
+    Q = {"g": g, "pe": g.tensor, "v": g.vector, "s": g.scalar, "sy": g.sync}
+    total, seen, done, pool = {}, {}, {}, [0]
+
+    def ev():
+        name = "e%d" % pool[0]
+        pool[0] += 1
+        total[name] = 0
+        return name
+
+    def sig(instr, name, k=1):
+        instr.then_inc(T.sem[name], k)
+        total[name] += k
+
+    def need(q, *names):
+        for name in names:
+            if done.get((q, name)) != total[name]:
+                Q[q].wait_ge(T.sem[name], total[name])
+                done[(q, name)] = total[name]
+                seen[name] = max(seen.get(name, 0), total[name])
+
+    total["a1"] = sum(_bits(m) for r in mine if r != rank for (_, _, qs, m) in pay_plan(r) if rank in qs) \
+        + sum(_bits(masks(r)[0]) for r in other)
+    total["a2"] = sum(_bits(m) for r in range(n) if r != rank for (_, _, _, qs, m) in d_plan(r) if rank in qs)
+    total["ls"] = 0
+
+    def send(parts):
+        trs = []
+        for src, dst, qs, m, sem in parts:
+            ids = []
+            for q in qs:
+                rid, pid = topo.addr(cores[q], core)
+                ids.append(DstId(rid=rid, pnc=pid))
+            trs.append(RemoteDMATransfer(dst_ids=ids, dma_engine_mask=m, remote_sem=T.sem[sem], srcs=[src],
+                                         dsts=[dst for _ in qs], alu_op=0))
+            total["ls"] += _bits(m)
+        g.remote_dma_fused(trs, local_sem=T.sem.ls)
+
+    P = [T.p0, T.p1]
+    pay = T.pay
+
+    ld_h, ld_w, ld_o = ev(), ev(), ev()
+    sig(g.sync.dma_start(T.hs[:], T.h[:]), ld_h, 16)
+    sig(g.scalar.dma_start(T.ws[:], T.w[:]), ld_w, 16)
+    sig(g.sync.dma_start(T.ohs[:], T.oh[:]), ld_o, 16)
+    e_io, e_sq, e_id = ev(), ev(), ev()
+    sig(g.iota(T.ramp[:], [[-1, 128]], 0, 1, allow_small_or_imprecise_dtypes=True), e_io)
+    need("s", e_io)
+    sig(g.scalar.activation(T.ramp[:], T.ramp[:], Square), e_sq)
+    need("s", e_sq)
+    sig(g.scalar.activation(T.ident[:], T.ramp[:], Exp, scale=-100.0), e_id)
+
+    e_z, e_nc, e_ex = [ev(), ev()], [ev(), ev()], [ev(), ev()]
+    need("pe", ld_h, ld_w)
+    for tb in range(2):
+        sig(g.tensor.matmul(P[tb][:, 0:256], T.hs[:, 128 * tb:128 * tb + 128], T.ws[:], True, True), e_z[tb])
+    e_tw = ev()
+    need("pe", e_id)
+    for vb in range(2):
+        sig(g.tensor.transpose(T.p2[:, 128 * vb:128 * vb + 128], T.ws[:, 128 * vb:128 * vb + 128], T.ident[:]), e_tw)
+    for tb in range(2):
+        c = base + ST + 2 * tb
+        need("v", e_z[tb])
+        sig(g.vector.tensor_reduce(pay[:, c:c + 1], P[tb][:, 0:256], X, AluOpType.max, negate=True), e_nc[tb])
+        need("s", e_z[tb], e_nc[tb])
+        sig(g.scalar.activation(T.eT[:, 256 * tb:256 * tb + 256], P[tb][:, 0:256], Exp, bias=pay[:, c:c + 1],
+                                accum_out=T.sacc[:, tb:tb + 1]), e_ex[tb])
+    e_wT, e_nid, e_st = ev(), ev(), ev()
+    need("v", e_tw)
+    sig(g.vector.tensor_copy(T.wT[:], T.p2[:, 0:256]), e_wT)
+    need("v", e_id)
+    sig(g.vector.tensor_scalar(T.nident[:], T.ident[:], -1.0, None, AluOpType.mult), e_nid)
+    need("v", e_ex[0], e_ex[1])
+    sig(g.vector.tensor_copy(pay[:, base + ST + 1:base + ST + 4:2], T.sacc[:, 0:2]), e_st)
+
+    need("g", e_nc[0], e_nc[1], e_st)
+    st = pay[:, base + ST:base + ST + 4]
+    send([(st, st, other, masks(rank)[0], "a1")])
+
+    e_te, e_e, e_u = [ev(), ev()], [ev(), ev()], [ev(), ev()]
+    PT = [T.p3, T.p4]
+    PU = [T.p5, T.p6]
+    for tb in range(2):
+        need("pe", e_ex[tb])
+        for vb in range(2):
+            c = 256 * tb + 128 * vb
+            sig(g.tensor.transpose(PT[tb][:, 128 * vb:128 * vb + 128], T.eT[:, c:c + 128], T.ident[:]), e_te[tb])
+        need("v", e_te[tb])
+        sig(g.vector.tensor_copy(T.e[:, 256 * tb:256 * tb + 256], PT[tb][:, 0:256]), e_e[tb])
+    e_pu, e_o, e_po = ev(), ev(), ev()
+    need("pe", e_wT)
+    for tb in range(2):
+        need("pe", e_e[tb])
+        for vb in range(2):
+            c = 256 * tb + 128 * vb
+            sig(g.tensor.matmul(PU[tb][:, 0:128], T.e[:, c:c + 128], T.wT[:, 128 * vb:128 * vb + 128], vb == 0, vb == 1),
+                e_u[tb])
+        need("v", e_u[tb])
+        c = base + U_COL[tb]
+        sig(g.vector.tensor_copy(pay[:, c:c + 128], PU[tb][:, 0:128]), e_pu)
+    need("pe", ld_o)
+    for vb in range(2):
+        sig(g.tensor.matmul(T.p7[:, 0:256], T.wT[:, 128 * vb:128 * vb + 128], T.ohs[:, 256 * vb:256 * vb + 256], vb == 0,
+                            vb == 1), e_o)
+    need("s", e_o)
+    for b in range(2):
+        c = base + O_COL[b]
+        sig(g.scalar.activation(pay[:, c:c + 128], T.p7[:, 128 * b:128 * b + 128], Copy), e_po)
+
+    need("g", e_pu, e_po)
+    send([(pay[:, base + a:base + z], pay[:, base + a:base + z], qs, m, "a1") for (a, z, qs, m) in pay_plan(rank)])
+
+    e_D = {}
+    for b in myb:
+        e_D[b] = ev()
+        need("pe", e_nid, e_po, e_nc[b], e_ex[b])
+        c = base + O_COL[b]
+        sig(g.tensor.matmul(P[b][:, 0:128], T.nident[:], pay[:, c:c + 128], True, False), e_D[b])
+    need("pe", "a1")
+    for b in myb:
+        for r in mine:
+            if r != rank:
+                c = SLOT * r + O_COL[b]
+                sig(g.tensor.matmul(P[b][:, 0:128], T.nident[:], pay[:, c:c + 128], False, False), e_D[b])
+    e_nM, e_E, e_T, e_S, e_R = [ev() for _ in myb], [ev() for _ in myb], [ev() for _ in myb], ev(), ev()
+    need("v", "a1", e_nc[0], e_nc[1], e_st)
+    for k, b in enumerate(myb):
+        sig(g.vector.tensor_reduce(T.nM[:, k:k + 1], pay[:, ST + 2 * b:n * SLOT:SLOT], X, AluOpType.min), e_nM[k])
+    need("s", "a1", e_nc[0], e_nc[1], e_st)
+    for k, b in enumerate(myb):
+        need("s", e_nM[k])
+        sig(g.scalar.activation(T.E[:, n * k:n * k + n], pay[:, ST + 2 * b:n * SLOT:SLOT], Exp, bias=T.nM[:, k:k + 1],
+                                scale=-1.0), e_E[k])
+    for k, b in enumerate(myb):
+        need("v", e_E[k])
+        sig(g.vector.tensor_tensor(T.Tm[:, n * k:n * k + n], T.E[:, n * k:n * k + n], pay[:, ST + 1 + 2 * b:n * SLOT:SLOT],
+                                   AluOpType.mult), e_T[k])
+        need("v", e_T[k])
+        sig(g.vector.tensor_reduce(T.S[:, k:k + 1], T.Tm[:, n * k:n * k + n], X, AluOpType.add), e_S)
+    need("v", e_S)
+    sig(g.vector.reciprocal(T.Rc[:, 0:nb], T.S[:, 0:nb]), e_R)
+    need("v", e_R, e_id)
+    e_snd = ev()
+    j = 0
+    for k, b in enumerate(myb):
+        for r in mine:
+            e_dg = ev()
+            sig(g.vector.tensor_scalar(T.dg[:, 128 * j:128 * j + 128], T.ident[:], T.E[:, n * k + r:n * k + r + 1],
+                                       T.Rc[:, k:k + 1], AluOpType.mult, AluOpType.mult), e_dg)
+            need("pe", e_dg, e_pu)
+            c = SLOT * r + U_COL[b]
+            sig(g.tensor.matmul(P[b][:, 0:128], pay[:, c:c + 128], T.dg[:, 128 * j:128 * j + 128], False, r == mine[-1]),
+                e_D[b])
+            j += 1
+    for k, b in enumerate(myb):
+        need("v", e_D[b])
+        sig(g.vector.tensor_copy(T.snd[:, 128 * k:128 * k + 128], P[b][:, 0:128]), e_snd)
+
+    need("g", e_snd)
+    send([(T.snd[:, 0:w], T[buf][:, a:a + w], qs, m, "a2") for (w, buf, a, qs, m) in d_plan(rank)])
+
+    e_out, e_sto = ev(), ev()
+    need("v", "a2")
+    for b in range(2):
+        own = P[b][:, 0:128] if b in myb else T.prt[:]
+        sig(g.vector.tensor_tensor(T.dout[:, 128 * b:128 * b + 128], own, T.rcv[:, 128 * b:128 * b + 128], AluOpType.add),
+            e_out)
+    need("sy", e_out)
+    sig(g.sync.dma_start(T.d[:], T.dout[:]), e_sto, 16)
+
+    for name in list(total):
+        if total[name] > seen.get(name, 0):
+            need("g", name)

@@ -1,7 +1,7 @@
 from concourse.bass import DstId, RemoteDMATransfer
 from concourse.mybir import AluOpType, AxisListType, ActivationFunctionType
 
-SLOT = 520
+SLOT = 512
 NEV = 72
 SCRATCH = {
     "hs": ("sbuf", [128, 256], "bfloat16"),
@@ -11,7 +11,8 @@ SCRATCH = {
     "ident": ("sbuf", [128, 128], "bfloat16"),
     "nident": ("sbuf", [128, 128], "bfloat16"),
     "eT": ("sbuf", [128, 512], "bfloat16"),
-    "sacc": ("sbuf", [128, 2], "float32"),
+    "ncb": ("sbuf", [128, 2], "bfloat16"),
+    "stf": ("sbuf", [128, 24], "float32"),
     "wT": ("sbuf", [128, 256], "bfloat16"),
     "e": ("sbuf", [128, 512], "bfloat16"),
     "pay": ("sbuf", [128, 6 * SLOT], "bfloat16"),
@@ -20,10 +21,10 @@ SCRATCH = {
     "Tm": ("sbuf", [128, 12], "float32"),
     "S": ("sbuf", [128, 2], "float32"),
     "Rc": ("sbuf", [128, 2], "float32"),
+    "dgE": ("sbuf", [128, 256], "bfloat16"),
     "dg": ("sbuf", [128, 512], "bfloat16"),
-    "snd": ("sbuf", [128, 256], "bfloat16"),
+    "loc": ("sbuf", [128, 256], "bfloat16"),
     "rcv": ("sbuf", [128, 256], "bfloat16"),
-    "prt": ("sbuf", [128, 128], "bfloat16"),
     "dout": ("sbuf", [128, 256], "bfloat16"),
     "p0": ("psum", [128, 512], "float32"),
     "p1": ("psum", [128, 512], "float32"),
@@ -34,11 +35,10 @@ SCRATCH = {
     "p6": ("psum", [128, 512], "float32"),
     "p7": ("psum", [128, 512], "float32"),
 }
-SEMAPHORES = ["a1", "a2", "ls"] + ["e%d" % i for i in range(NEV)]
+SEMAPHORES = ["a0", "a1", "a2", "a3", "ls"] + ["e%d" % i for i in range(NEV)]
 
-O_COL = (0, 388)
-U_COL = (128, 260)
-ST = 256
+U_COL = (0, 384)
+O_COL = (128, 256)
 
 
 def _bits(m):
@@ -52,6 +52,7 @@ def rank_program(g, core, T, topo):
     cores = list(T.cores)
     n = len(cores)
     Exp, Square, Copy = ActivationFunctionType.Exp, ActivationFunctionType.Square, ActivationFunctionType.Copy
+    Identity = ActivationFunctionType.Identity
     X = AxisListType.X
 
     def place(r):
@@ -74,12 +75,16 @@ def rank_program(g, core, T, topo):
         on = topo.mask(cores[r], cores[[q for q in mine_of(r) if q != r][0]])
         return off, on & ~off, on & off
 
+    def stat_mask(r):
+        off, stay, both = masks(r)
+        return stay | both if len(mine_of(r)) > 2 else stay
+
     def pay_plan(r):
         by = {}
         for q in mine_of(r):
             if q != r:
                 bl = blocks_of(q)
-                rng = (0, 516) if len(bl) == 2 else ((0, 258) if bl[0] == 0 else (258, 516))
+                rng = (0, 512) if len(bl) == 2 else (256 * bl[0], 256 * bl[0] + 256)
                 by.setdefault(rng, []).append(q)
         items = sorted(by.items(), key=lambda kv: -len(kv[1]))
         off, stay, both = masks(r)
@@ -89,11 +94,12 @@ def rank_program(g, core, T, topo):
         off, stay, both = masks(r)
         i = mine_of(r).index(r)
         if half(r):
-            b = i % 2
-            return [(128, "rcv", 128 * b, [other_of(r)[i // 2]], off), (128, "prt", 0, [mine_of(r)[i ^ 1]], stay)]
-        return [(256, "rcv", 0, other_of(r)[2 * i:2 * i + 2], off)]
+            a = 128 * (i % 2)
+            return [(a, a + 128, "rcv", [other_of(r)[i // 2]], off, "a2"), (a, a + 128, "loc", [mine_of(r)[i ^ 1]], stay, "a3")]
+        return [(0, 256, "rcv", other_of(r)[2 * i:2 * i + 2], off, "a2")]
 
     mine, other, myb = mine_of(rank), other_of(rank), blocks_of(rank)
+    peers = [r for r in mine if r != rank]
     nb = len(myb)
     base = SLOT * rank
 
@@ -112,14 +118,16 @@ def rank_program(g, core, T, topo):
 
     def need(q, *names):
         for name in names:
-            if done.get((q, name)) != total[name]:
+            if total[name] and done.get((q, name)) != total[name]:
                 Q[q].wait_ge(T.sem[name], total[name])
                 done[(q, name)] = total[name]
                 seen[name] = max(seen.get(name, 0), total[name])
 
-    total["a1"] = sum(_bits(m) for r in mine if r != rank for (_, _, qs, m) in pay_plan(r) if rank in qs) \
-        + sum(_bits(masks(r)[0]) for r in other)
-    total["a2"] = sum(_bits(m) for r in range(n) if r != rank for (_, _, _, qs, m) in d_plan(r) if rank in qs)
+    total["a0"] = sum(_bits(masks(r)[0]) for r in other) + sum(_bits(stat_mask(r)) for r in peers)
+    total["a1"] = sum(_bits(m) for r in peers for (_, _, qs, m) in pay_plan(r) if rank in qs)
+    for name in ("a2", "a3"):
+        total[name] = sum(_bits(m) for r in range(n) if r != rank for (_, _, _, qs, m, sem) in d_plan(r)
+                          if rank in qs and sem == name)
     total["ls"] = 0
 
     def send(parts):
@@ -135,7 +143,7 @@ def rank_program(g, core, T, topo):
         g.remote_dma_fused(trs, local_sem=T.sem.ls)
 
     P = [T.p0, T.p1]
-    pay = T.pay
+    pay, stf = T.pay, T.stf
 
     ld_h, ld_w, ld_o = ev(), ev(), ev()
     sig(g.sync.dma_start(T.hs[:], T.h[:]), ld_h, 16)
@@ -157,23 +165,25 @@ def rank_program(g, core, T, topo):
     for vb in range(2):
         sig(g.tensor.transpose(T.p2[:, 128 * vb:128 * vb + 128], T.ws[:, 128 * vb:128 * vb + 128], T.ident[:]), e_tw)
     for tb in range(2):
-        c = base + ST + 2 * tb
+        c = 4 * rank + 2 * tb + 1
         need("v", e_z[tb])
-        sig(g.vector.tensor_reduce(pay[:, c:c + 1], P[tb][:, 0:256], X, AluOpType.max, negate=True), e_nc[tb])
+        sig(g.vector.tensor_reduce(T.ncb[:, tb:tb + 1], P[tb][:, 0:256], X, AluOpType.max, negate=True), e_nc[tb])
         need("s", e_z[tb], e_nc[tb])
-        sig(g.scalar.activation(T.eT[:, 256 * tb:256 * tb + 256], P[tb][:, 0:256], Exp, bias=pay[:, c:c + 1],
-                                accum_out=T.sacc[:, tb:tb + 1]), e_ex[tb])
-    e_wT, e_nid, e_st = ev(), ev(), ev()
+        sig(g.scalar.activation(T.eT[:, 256 * tb:256 * tb + 256], P[tb][:, 0:256], Exp, bias=T.ncb[:, tb:tb + 1],
+                                accum_out=stf[:, c:c + 1]), e_ex[tb])
+    e_st = ev()
+    need("v", e_nc[0], e_nc[1])
+    sig(g.vector.tensor_copy(stf[:, 4 * rank:4 * rank + 3:2], T.ncb[:, 0:2]), e_st)
+    e_wT, e_nid = ev(), ev()
     need("v", e_tw)
     sig(g.vector.tensor_copy(T.wT[:], T.p2[:, 0:256]), e_wT)
     need("v", e_id)
     sig(g.vector.tensor_scalar(T.nident[:], T.ident[:], -1.0, None, AluOpType.mult), e_nid)
-    need("v", e_ex[0], e_ex[1])
-    sig(g.vector.tensor_copy(pay[:, base + ST + 1:base + ST + 4:2], T.sacc[:, 0:2]), e_st)
 
-    need("g", e_nc[0], e_nc[1], e_st)
-    st = pay[:, base + ST:base + ST + 4]
-    send([(st, st, other, masks(rank)[0], "a1")])
+    need("g", e_ex[0], e_ex[1], e_st)
+    st = stf[:, 4 * rank:4 * rank + 4]
+    send([(st, st, other, masks(rank)[0], "a0")])
+    send([(st, st, peers, stat_mask(rank), "a0")])
 
     e_te, e_e, e_u = [ev(), ev()], [ev(), ev()], [ev(), ev()]
     PT = [T.p3, T.p4]
@@ -186,7 +196,12 @@ def rank_program(g, core, T, topo):
         need("v", e_te[tb])
         sig(g.vector.tensor_copy(T.e[:, 256 * tb:256 * tb + 256], PT[tb][:, 0:256]), e_e[tb])
     e_pu, e_o, e_po = ev(), ev(), ev()
-    need("pe", e_wT)
+    need("pe", e_wT, ld_o)
+    for vb in range(2):
+        sig(g.tensor.matmul(T.p7[:, 0:256], T.wT[:, 128 * vb:128 * vb + 128], T.ohs[:, 256 * vb:256 * vb + 256], vb == 0,
+                            vb == 1), e_o)
+    need("s", e_o)
+    sig(g.scalar.activation(pay[:, base + O_COL[0]:base + O_COL[0] + 256], T.p7[:, 0:256], Copy), e_po)
     for tb in range(2):
         need("pe", e_e[tb])
         for vb in range(2):
@@ -196,73 +211,85 @@ def rank_program(g, core, T, topo):
         need("v", e_u[tb])
         c = base + U_COL[tb]
         sig(g.vector.tensor_copy(pay[:, c:c + 128], PU[tb][:, 0:128]), e_pu)
-    need("pe", ld_o)
-    for vb in range(2):
-        sig(g.tensor.matmul(T.p7[:, 0:256], T.wT[:, 128 * vb:128 * vb + 128], T.ohs[:, 256 * vb:256 * vb + 256], vb == 0,
-                            vb == 1), e_o)
-    need("s", e_o)
-    for b in range(2):
-        c = base + O_COL[b]
-        sig(g.scalar.activation(pay[:, c:c + 128], T.p7[:, 128 * b:128 * b + 128], Copy), e_po)
 
     need("g", e_pu, e_po)
     send([(pay[:, base + a:base + z], pay[:, base + a:base + z], qs, m, "a1") for (a, z, qs, m) in pay_plan(rank)])
 
-    e_D = {}
-    for b in myb:
-        e_D[b] = ev()
-        need("pe", e_nid, e_po, e_nc[b], e_ex[b])
-        c = base + O_COL[b]
-        sig(g.tensor.matmul(P[b][:, 0:128], T.nident[:], pay[:, c:c + 128], True, False), e_D[b])
-    need("pe", "a1")
-    for b in myb:
-        for r in mine:
-            if r != rank:
-                c = SLOT * r + O_COL[b]
-                sig(g.tensor.matmul(P[b][:, 0:128], T.nident[:], pay[:, c:c + 128], False, False), e_D[b])
+    stats_in = ["a0", e_ex[0], e_ex[1], e_st]
     e_nM, e_E, e_T, e_S, e_R = [ev() for _ in myb], [ev() for _ in myb], [ev() for _ in myb], ev(), ev()
-    need("v", "a1", e_nc[0], e_nc[1], e_st)
+    need("v", *stats_in)
     for k, b in enumerate(myb):
-        sig(g.vector.tensor_reduce(T.nM[:, k:k + 1], pay[:, ST + 2 * b:n * SLOT:SLOT], X, AluOpType.min), e_nM[k])
-    need("s", "a1", e_nc[0], e_nc[1], e_st)
+        sig(g.vector.tensor_reduce(T.nM[:, k:k + 1], stf[:, 2 * b:4 * n:4], X, AluOpType.min), e_nM[k])
+    need("s", *stats_in)
     for k, b in enumerate(myb):
         need("s", e_nM[k])
-        sig(g.scalar.activation(T.E[:, n * k:n * k + n], pay[:, ST + 2 * b:n * SLOT:SLOT], Exp, bias=T.nM[:, k:k + 1],
+        sig(g.scalar.activation(T.E[:, n * k:n * k + n], stf[:, 2 * b:4 * n:4], Exp, bias=T.nM[:, k:k + 1],
                                 scale=-1.0), e_E[k])
+    us = [(rank, k, b) for k, b in enumerate(myb)] + [(r, k, b) for k, b in enumerate(myb) for r in peers]
+    e_dg, e_pre, dcol = {}, {}, {}
+    for j, (r, k, b) in enumerate(us):
+        e_dg[(r, b)], dcol[(r, b)] = ev(), 128 * j
+        if j % 2:
+            e_pre[(r, b)] = ev()
+            need("s", e_E[k], e_id)
+            sig(g.scalar.activation(T.dgE[:, 64 * (j - 1):64 * (j - 1) + 128], T.ident[:], Identity,
+                                    scale=T.E[:, n * k + r:n * k + r + 1]), e_pre[(r, b)])
     for k, b in enumerate(myb):
         need("v", e_E[k])
-        sig(g.vector.tensor_tensor(T.Tm[:, n * k:n * k + n], T.E[:, n * k:n * k + n], pay[:, ST + 1 + 2 * b:n * SLOT:SLOT],
+        sig(g.vector.tensor_tensor(T.Tm[:, n * k:n * k + n], T.E[:, n * k:n * k + n], stf[:, 2 * b + 1:4 * n:4],
                                    AluOpType.mult), e_T[k])
+    for k, b in enumerate(myb):
         need("v", e_T[k])
         sig(g.vector.tensor_reduce(T.S[:, k:k + 1], T.Tm[:, n * k:n * k + n], X, AluOpType.add), e_S)
     need("v", e_S)
     sig(g.vector.reciprocal(T.Rc[:, 0:nb], T.S[:, 0:nb]), e_R)
     need("v", e_R, e_id)
-    e_snd = ev()
-    j = 0
-    for k, b in enumerate(myb):
-        for r in mine:
-            e_dg = ev()
-            sig(g.vector.tensor_scalar(T.dg[:, 128 * j:128 * j + 128], T.ident[:], T.E[:, n * k + r:n * k + r + 1],
-                                       T.Rc[:, k:k + 1], AluOpType.mult, AluOpType.mult), e_dg)
-            need("pe", e_dg, e_pu)
+    for j, (r, k, b) in enumerate(us):
+        out = T.dg[:, dcol[(r, b)]:dcol[(r, b)] + 128]
+        if j % 2:
+            need("s", e_R, e_pre[(r, b)])
+            sig(g.scalar.activation(out, T.dgE[:, 64 * (j - 1):64 * (j - 1) + 128], Identity, scale=T.Rc[:, k:k + 1]),
+                e_dg[(r, b)])
+        else:
+            sig(g.vector.tensor_scalar(out, T.ident[:], T.E[:, n * k + r:n * k + r + 1], T.Rc[:, k:k + 1], AluOpType.mult,
+                                       AluOpType.mult), e_dg[(r, b)])
+
+    order = [("o", rank, b) for b in myb] + [("o", r, b) for b in myb for r in peers] + [("u", r, b) for (r, k, b) in us]
+    e_D = {b: ev() for b in myb}
+    left = {b: 2 * len(mine) for b in myb}
+    need("pe", e_nid, e_po, e_pu)
+    for kind, r, b in order:
+        if r != rank:
+            need("pe", "a1")
+        first = left[b] == 2 * len(mine)
+        left[b] -= 1
+        if first:
+            need("pe", e_nc[b], e_ex[b])
+        if kind == "o":
+            c = SLOT * r + O_COL[b]
+            sig(g.tensor.matmul(P[b][:, 0:128], T.nident[:], pay[:, c:c + 128], first, left[b] == 0), e_D[b])
+        else:
+            need("pe", e_dg[(r, b)])
             c = SLOT * r + U_COL[b]
-            sig(g.tensor.matmul(P[b][:, 0:128], pay[:, c:c + 128], T.dg[:, 128 * j:128 * j + 128], False, r == mine[-1]),
-                e_D[b])
-            j += 1
+            sig(g.tensor.matmul(P[b][:, 0:128], pay[:, c:c + 128], T.dg[:, dcol[(r, b)]:dcol[(r, b)] + 128], first,
+                                left[b] == 0), e_D[b])
+    e_snd = ev()
     for k, b in enumerate(myb):
-        need("v", e_D[b])
-        sig(g.vector.tensor_copy(T.snd[:, 128 * k:128 * k + 128], P[b][:, 0:128]), e_snd)
+        if k == 0:
+            need("v", e_D[b])
+            sig(g.vector.tensor_copy(T.loc[:, 128 * b:128 * b + 128], P[b][:, 0:128]), e_snd)
+        else:
+            need("s", e_D[b])
+            sig(g.scalar.activation(T.loc[:, 128 * b:128 * b + 128], P[b][:, 0:128], Copy), e_snd)
 
     need("g", e_snd)
-    send([(T.snd[:, 0:w], T[buf][:, a:a + w], qs, m, "a2") for (w, buf, a, qs, m) in d_plan(rank)])
+    send([(T.loc[:, a:z], T[buf][:, a:z], qs, m, sem) for (a, z, buf, qs, m, sem) in d_plan(rank)])
 
-    e_out, e_sto = ev(), ev()
-    need("v", "a2")
-    for b in range(2):
-        own = P[b][:, 0:128] if b in myb else T.prt[:]
-        sig(g.vector.tensor_tensor(T.dout[:, 128 * b:128 * b + 128], own, T.rcv[:, 128 * b:128 * b + 128], AluOpType.add),
-            e_out)
+    e_pf, e_out, e_sto = ev(), ev(), ev()
+    need("pe", e_snd, "a3", e_o, e_po, e_id)
+    sig(g.tensor.matmul(T.p7[:, 0:256], T.ident[:], T.loc[:], True, True), e_pf)
+    need("v", "a2", e_pf)
+    sig(g.vector.tensor_tensor(T.dout[:], T.p7[:, 0:256], T.rcv[:], AluOpType.add), e_out)
     need("sy", e_out)
     sig(g.sync.dma_start(T.d[:], T.dout[:]), e_sto, 16)
 

from concourse.bass import DstId, RemoteDMATransfer
from concourse.mybir import AluOpType, AxisListType, ActivationFunctionType

SLOT = 512
NEV = 72
SCRATCH = {
    "hs": ("sbuf", [128, 256], "bfloat16"),
    "ws": ("sbuf", [128, 256], "bfloat16"),
    "ohs": ("sbuf", [128, 512], "bfloat16"),
    "ramp": ("sbuf", [128, 128], "float32"),
    "ident": ("sbuf", [128, 128], "bfloat16"),
    "nident": ("sbuf", [128, 128], "bfloat16"),
    "eT": ("sbuf", [128, 512], "bfloat16"),
    "ncb": ("sbuf", [128, 2], "bfloat16"),
    "stf": ("sbuf", [128, 24], "float32"),
    "wT": ("sbuf", [128, 256], "bfloat16"),
    "e": ("sbuf", [128, 512], "bfloat16"),
    "pay": ("sbuf", [128, 6 * SLOT], "bfloat16"),
    "nM": ("sbuf", [128, 2], "float32"),
    "E": ("sbuf", [128, 12], "float32"),
    "Tm": ("sbuf", [128, 12], "float32"),
    "S": ("sbuf", [128, 2], "float32"),
    "Rc": ("sbuf", [128, 2], "float32"),
    "dgE": ("sbuf", [128, 256], "bfloat16"),
    "dg": ("sbuf", [128, 512], "bfloat16"),
    "loc": ("sbuf", [128, 256], "bfloat16"),
    "rcv": ("sbuf", [128, 256], "bfloat16"),
    "dout": ("sbuf", [128, 256], "bfloat16"),
    "p0": ("psum", [128, 512], "float32"),
    "p1": ("psum", [128, 512], "float32"),
    "p2": ("psum", [128, 1024], "bfloat16"),
    "p3": ("psum", [128, 1024], "bfloat16"),
    "p4": ("psum", [128, 1024], "bfloat16"),
    "p5": ("psum", [128, 512], "float32"),
    "p6": ("psum", [128, 512], "float32"),
    "p7": ("psum", [128, 512], "float32"),
}
SEMAPHORES = ["a0", "a1", "a2", "a3", "ls"] + ["e%d" % i for i in range(NEV)]

U_COL = (0, 384)
O_COL = (128, 256)


def _bits(m):
    return bin(m).count("1")


def rank_program(g, core, T, topo):
    rank = T.rank_of(core)
    if rank is None:
        return
    cores = list(T.cores)
    n = len(cores)
    Exp, Square, Copy = ActivationFunctionType.Exp, ActivationFunctionType.Square, ActivationFunctionType.Copy
    Identity = ActivationFunctionType.Identity
    X = AxisListType.X

    def place(r):
        return (topo.host(cores[r]), topo.chip(cores[r]))

    def mine_of(r):
        return [q for q in range(n) if place(q) == place(r)]

    def other_of(r):
        return [q for q in range(n) if place(q) != place(r)]

    def half(r):
        return len(mine_of(r)) == 2 * len(other_of(r))

    def blocks_of(r):
        return [mine_of(r).index(r) % 2] if half(r) else [0, 1]

    def masks(r):
        off = topo.mask(cores[r], cores[other_of(r)[0]])
        on = topo.mask(cores[r], cores[[q for q in mine_of(r) if q != r][0]])
        return off, on & ~off, on & off

    def stat_mask(r):
        off, stay, both = masks(r)
        return stay | both if len(mine_of(r)) > 2 else stay

    def pay_plan(r):
        by = {}
        for q in mine_of(r):
            if q != r:
                bl = blocks_of(q)
                rng = (0, 512) if len(bl) == 2 else (256 * bl[0], 256 * bl[0] + 256)
                by.setdefault(rng, []).append(q)
        items = sorted(by.items(), key=lambda kv: -len(kv[1]))
        off, stay, both = masks(r)
        return [(rng[0], rng[1], qs, (stay, both)[i]) for i, (rng, qs) in enumerate(items)]

    def d_plan(r):
        off, stay, both = masks(r)
        i = mine_of(r).index(r)
        if half(r):
            a = 128 * (i % 2)
            return [(a, a + 128, "rcv", [other_of(r)[i // 2]], off, "a2"), (a, a + 128, "loc", [mine_of(r)[i ^ 1]], stay, "a3")]
        return [(0, 256, "rcv", other_of(r)[2 * i:2 * i + 2], off, "a2")]

    mine, other, myb = mine_of(rank), other_of(rank), blocks_of(rank)
    peers = [r for r in mine if r != rank]
    nb = len(myb)
    base = SLOT * rank

    Q = {"g": g, "pe": g.tensor, "v": g.vector, "s": g.scalar, "sy": g.sync}
    total, seen, done, pool = {}, {}, {}, [0]

    def ev():
        name = "e%d" % pool[0]
        pool[0] += 1
        total[name] = 0
        return name

    def sig(instr, name, k=1):
        instr.then_inc(T.sem[name], k)
        total[name] += k

    def need(q, *names):
        for name in names:
            if total[name] and done.get((q, name)) != total[name]:
                Q[q].wait_ge(T.sem[name], total[name])
                done[(q, name)] = total[name]
                seen[name] = max(seen.get(name, 0), total[name])

    total["a0"] = sum(_bits(masks(r)[0]) for r in other) + sum(_bits(stat_mask(r)) for r in peers)
    total["a1"] = sum(_bits(m) for r in peers for (_, _, qs, m) in pay_plan(r) if rank in qs)
    for name in ("a2", "a3"):
        total[name] = sum(_bits(m) for r in range(n) if r != rank for (_, _, _, qs, m, sem) in d_plan(r)
                          if rank in qs and sem == name)
    total["ls"] = 0

    def send(parts):
        trs = []
        for src, dst, qs, m, sem in parts:
            ids = []
            for q in qs:
                rid, pid = topo.addr(cores[q], core)
                ids.append(DstId(rid=rid, pnc=pid))
            trs.append(RemoteDMATransfer(dst_ids=ids, dma_engine_mask=m, remote_sem=T.sem[sem], srcs=[src],
                                         dsts=[dst for _ in qs], alu_op=0))
            total["ls"] += _bits(m)
        g.remote_dma_fused(trs, local_sem=T.sem.ls)

    P = [T.p0, T.p1]
    pay, stf = T.pay, T.stf

    ld_h, ld_w, ld_o = ev(), ev(), ev()
    sig(g.sync.dma_start(T.hs[:], T.h[:]), ld_h, 16)
    sig(g.scalar.dma_start(T.ws[:], T.w[:]), ld_w, 16)
    sig(g.sync.dma_start(T.ohs[:], T.oh[:]), ld_o, 16)
    e_io, e_sq, e_id = ev(), ev(), ev()
    sig(g.iota(T.ramp[:], [[-1, 128]], 0, 1, allow_small_or_imprecise_dtypes=True), e_io)
    need("s", e_io)
    sig(g.scalar.activation(T.ramp[:], T.ramp[:], Square), e_sq)
    need("s", e_sq)
    sig(g.scalar.activation(T.ident[:], T.ramp[:], Exp, scale=-100.0), e_id)

    e_z, e_nc, e_ex = [ev(), ev()], [ev(), ev()], [ev(), ev()]
    need("pe", ld_h, ld_w)
    for tb in range(2):
        sig(g.tensor.matmul(P[tb][:, 0:256], T.hs[:, 128 * tb:128 * tb + 128], T.ws[:], True, True), e_z[tb])
    e_tw = ev()
    need("pe", e_id)
    for vb in range(2):
        sig(g.tensor.transpose(T.p2[:, 128 * vb:128 * vb + 128], T.ws[:, 128 * vb:128 * vb + 128], T.ident[:]), e_tw)
    for tb in range(2):
        c = 4 * rank + 2 * tb + 1
        need("v", e_z[tb])
        sig(g.vector.tensor_reduce(T.ncb[:, tb:tb + 1], P[tb][:, 0:256], X, AluOpType.max, negate=True), e_nc[tb])
        need("s", e_z[tb], e_nc[tb])
        sig(g.scalar.activation(T.eT[:, 256 * tb:256 * tb + 256], P[tb][:, 0:256], Exp, bias=T.ncb[:, tb:tb + 1],
                                accum_out=stf[:, c:c + 1]), e_ex[tb])
    e_st = ev()
    need("v", e_nc[0], e_nc[1])
    sig(g.vector.tensor_copy(stf[:, 4 * rank:4 * rank + 3:2], T.ncb[:, 0:2]), e_st)
    e_wT, e_nid = ev(), ev()
    need("v", e_tw)
    sig(g.vector.tensor_copy(T.wT[:], T.p2[:, 0:256]), e_wT)
    need("v", e_id)
    sig(g.vector.tensor_scalar(T.nident[:], T.ident[:], -1.0, None, AluOpType.mult), e_nid)

    need("g", e_ex[0], e_ex[1], e_st)
    st = stf[:, 4 * rank:4 * rank + 4]
    send([(st, st, other, masks(rank)[0], "a0")])
    send([(st, st, peers, stat_mask(rank), "a0")])

    e_te, e_e, e_u = [ev(), ev()], [ev(), ev()], [ev(), ev()]
    PT = [T.p3, T.p4]
    PU = [T.p5, T.p6]
    for tb in range(2):
        need("pe", e_ex[tb])
        for vb in range(2):
            c = 256 * tb + 128 * vb
            sig(g.tensor.transpose(PT[tb][:, 128 * vb:128 * vb + 128], T.eT[:, c:c + 128], T.ident[:]), e_te[tb])
        need("v", e_te[tb])
        sig(g.vector.tensor_copy(T.e[:, 256 * tb:256 * tb + 256], PT[tb][:, 0:256]), e_e[tb])
    e_pu, e_o, e_po = ev(), ev(), ev()
    need("pe", e_wT, ld_o)
    for vb in range(2):
        sig(g.tensor.matmul(T.p7[:, 0:256], T.wT[:, 128 * vb:128 * vb + 128], T.ohs[:, 256 * vb:256 * vb + 256], vb == 0,
                            vb == 1), e_o)
    need("s", e_o)
    sig(g.scalar.activation(pay[:, base + O_COL[0]:base + O_COL[0] + 256], T.p7[:, 0:256], Copy), e_po)
    for tb in range(2):
        need("pe", e_e[tb])
        for vb in range(2):
            c = 256 * tb + 128 * vb
            sig(g.tensor.matmul(PU[tb][:, 0:128], T.e[:, c:c + 128], T.wT[:, 128 * vb:128 * vb + 128], vb == 0, vb == 1),
                e_u[tb])
        need("v", e_u[tb])
        c = base + U_COL[tb]
        sig(g.vector.tensor_copy(pay[:, c:c + 128], PU[tb][:, 0:128]), e_pu)

    need("g", e_pu, e_po)
    send([(pay[:, base + a:base + z], pay[:, base + a:base + z], qs, m, "a1") for (a, z, qs, m) in pay_plan(rank)])

    stats_in = ["a0", e_ex[0], e_ex[1], e_st]
    e_nM, e_E, e_T, e_S, e_R = [ev() for _ in myb], [ev() for _ in myb], [ev() for _ in myb], ev(), ev()
    need("v", *stats_in)
    for k, b in enumerate(myb):
        sig(g.vector.tensor_reduce(T.nM[:, k:k + 1], stf[:, 2 * b:4 * n:4], X, AluOpType.min), e_nM[k])
    need("s", *stats_in)
    for k, b in enumerate(myb):
        need("s", e_nM[k])
        sig(g.scalar.activation(T.E[:, n * k:n * k + n], stf[:, 2 * b:4 * n:4], Exp, bias=T.nM[:, k:k + 1],
                                scale=-1.0), e_E[k])
    us = [(rank, k, b) for k, b in enumerate(myb)] + [(r, k, b) for k, b in enumerate(myb) for r in peers]
    e_dg, e_pre, dcol = {}, {}, {}
    for j, (r, k, b) in enumerate(us):
        e_dg[(r, b)], dcol[(r, b)] = ev(), 128 * j
        if j % 2:
            e_pre[(r, b)] = ev()
            need("s", e_E[k], e_id)
            sig(g.scalar.activation(T.dgE[:, 64 * (j - 1):64 * (j - 1) + 128], T.ident[:], Identity,
                                    scale=T.E[:, n * k + r:n * k + r + 1]), e_pre[(r, b)])
    for k, b in enumerate(myb):
        need("v", e_E[k])
        sig(g.vector.tensor_tensor(T.Tm[:, n * k:n * k + n], T.E[:, n * k:n * k + n], stf[:, 2 * b + 1:4 * n:4],
                                   AluOpType.mult), e_T[k])
    for k, b in enumerate(myb):
        need("v", e_T[k])
        sig(g.vector.tensor_reduce(T.S[:, k:k + 1], T.Tm[:, n * k:n * k + n], X, AluOpType.add), e_S)
    need("v", e_S)
    sig(g.vector.reciprocal(T.Rc[:, 0:nb], T.S[:, 0:nb]), e_R)
    need("v", e_R, e_id)
    for j, (r, k, b) in enumerate(us):
        out = T.dg[:, dcol[(r, b)]:dcol[(r, b)] + 128]
        if j % 2:
            need("s", e_R, e_pre[(r, b)])
            sig(g.scalar.activation(out, T.dgE[:, 64 * (j - 1):64 * (j - 1) + 128], Identity, scale=T.Rc[:, k:k + 1]),
                e_dg[(r, b)])
        else:
            sig(g.vector.tensor_scalar(out, T.ident[:], T.E[:, n * k + r:n * k + r + 1], T.Rc[:, k:k + 1], AluOpType.mult,
                                       AluOpType.mult), e_dg[(r, b)])

    order = [("o", rank, b) for b in myb] + [("o", r, b) for b in myb for r in peers] + [("u", r, b) for (r, k, b) in us]
    e_D = {b: ev() for b in myb}
    left = {b: 2 * len(mine) for b in myb}
    need("pe", e_nid, e_po, e_pu)
    for kind, r, b in order:
        if r != rank:
            need("pe", "a1")
        first = left[b] == 2 * len(mine)
        left[b] -= 1
        if first:
            need("pe", e_nc[b], e_ex[b])
        if kind == "o":
            c = SLOT * r + O_COL[b]
            sig(g.tensor.matmul(P[b][:, 0:128], T.nident[:], pay[:, c:c + 128], first, left[b] == 0), e_D[b])
        else:
            need("pe", e_dg[(r, b)])
            c = SLOT * r + U_COL[b]
            sig(g.tensor.matmul(P[b][:, 0:128], pay[:, c:c + 128], T.dg[:, dcol[(r, b)]:dcol[(r, b)] + 128], first,
                                left[b] == 0), e_D[b])
    e_snd = ev()
    for k, b in enumerate(myb):
        if k == 0:
            need("v", e_D[b])
            sig(g.vector.tensor_copy(T.loc[:, 128 * b:128 * b + 128], P[b][:, 0:128]), e_snd)
        else:
            need("s", e_D[b])
            sig(g.scalar.activation(T.loc[:, 128 * b:128 * b + 128], P[b][:, 0:128], Copy), e_snd)

    need("g", e_snd)
    send([(T.loc[:, a:z], T[buf][:, a:z], qs, m, sem) for (a, z, buf, qs, m, sem) in d_plan(rank)])

    e_pf, e_out, e_sto = ev(), ev(), ev()
    need("pe", e_snd, "a3", e_o, e_po, e_id)
    sig(g.tensor.matmul(T.p7[:, 0:256], T.ident[:], T.loc[:], True, True), e_pf)
    need("v", "a2", e_pf)
    sig(g.vector.tensor_tensor(T.dout[:], T.p7[:, 0:256], T.rcv[:], AluOpType.add), e_out)
    need("sy", e_out)
    sig(g.sync.dma_start(T.d[:], T.dout[:]), e_sto, 16)

    for name in list(total):
        if total[name] > seen.get(name, 0):
            need("g", name)
